import numpy as np
import ml_dtypes


def mxq(x, axis, fmt="e4m3"):
    dtype, down = {"e4m3": (ml_dtypes.float8_e4m3fn, 7), "e5m2": (ml_dtypes.float8_e5m2, 14)}[fmt]
    v = np.moveaxis(np.asarray(x, np.float32).astype(ml_dtypes.bfloat16).astype(np.float64), axis, -1)
    blocks = v.reshape(v.shape[:-1] + (-1, 32))
    amax = np.abs(blocks).max(-1, keepdims=True)
    byte = np.maximum(np.where(amax > 0, np.frexp(amax)[1] - 1 + 127, 0) - down, 1)
    scale = np.exp2(byte - 127.0)
    codes = (blocks / scale).astype(np.float32).astype(dtype).astype(np.float64)
    return np.moveaxis((codes * scale).reshape(v.shape), -1, axis)


WIDE = False


def mx_kscale(k):
    if not WIDE:
        return np.ones(k)
    levels = np.array([10, -10, 5, -5, 0])
    if k % 512:
        return np.exp2(np.random.permutation(np.resize(levels, k // 32))).repeat(32)
    a = np.empty((k // 512, 16))
    for p in range(k // 512):
        a[p, :8] = np.random.permutation(np.resize(levels, 8))
        for g in range(8):
            far = levels[np.abs(levels - a[p, g]) >= 10]
            a[p, g + 8] = far[np.random.randint(len(far))]
    return np.exp2(a.ravel()).repeat(32)


def f64(x):
    return np.asarray(x).astype(np.float64)


def striped(idx):
    return np.tile(np.asarray(idx).reshape(-1, 16).T, (8, 1)).astype(np.uint16)


def unstriped(offs):
    return offs[:16].T.reshape(-1).astype(np.int64)


E2M1 = np.array([0.0, 0.5, 1.0, 1.5, 2.0, 3.0, 4.0, 6.0, -0.0, -0.5, -1.0, -1.5, -2.0, -3.0, -4.0, -6.0])


def pack_weight(w, fmt):
    k, n = w.shape
    w = f64(np.asarray(w, np.float32).astype(ml_dtypes.bfloat16)).reshape(k // 32, 32, n)
    amax = np.abs(w).max(1)
    if fmt == "e4m3":
        byte = np.frexp(amax)[1] - 1 + 127 - 7
    else:
        mant, ex = np.frexp(amax / 6.0)
        byte = np.where(mant > 0.5, ex, ex - 1) + 127
    byte = np.clip(np.where(amax > 0, byte, 1), 1, 254)
    scaled = (w * np.exp2(127.0 - byte)[:, None, :]).reshape(k, n).astype(np.float32)
    by_word = np.ascontiguousarray(scaled.reshape(k // 512, 128, 4, n).transpose(0, 1, 3, 2))
    if fmt == "e4m3":
        words = by_word.astype(ml_dtypes.float8_e4m3fn).view(np.uint8)
    else:
        c = by_word.astype(ml_dtypes.float4_e2m1fn).view(np.uint8) & 0xF
        words = (c[..., 0::2] | (c[..., 1::2] << 4)).reshape(k // 512, 128, 2 * n)
    return np.ascontiguousarray(words), np.ascontiguousarray(byte.astype(np.uint8).reshape(k // 512, 16, n))


def unpack_weight(words, scales, fmt):
    g, _, n = scales.shape
    words = np.ascontiguousarray(words).reshape(g, 128, n, -1)
    if fmt == "e4m3":
        vals = words.view(ml_dtypes.float8_e4m3fn).astype(np.float64)
    else:
        nib = np.empty((g, 128, n, 4), np.uint8)
        nib[..., 0::2] = words & 0xF
        nib[..., 1::2] = words >> 4
        vals = E2M1[nib]
    vals = vals * np.repeat(np.exp2(scales.astype(np.float64) - 127.0), 8, axis=1)[..., None]
    return vals.transpose(0, 1, 3, 2).reshape(g * 512, n)


def sgn(shape):
    return np.random.uniform(0.5, 2.0, shape) * np.where(np.random.standard_normal(shape) < 0, -1.0, 1.0)


K, T, J, R, F, Z, C, S, O, U = 512, 1024, 256, 512, 512, 1024, 512, 512, 128, 128


def setup_inputs():
    n = np.random.standard_normal
    idx = np.random.permutation(T)[:J]
    idx2 = np.random.permutation(Z)[:J]
    idx3 = np.random.permutation(C)[:J]
    idx4 = np.random.permutation(S)[:O]
    idx5 = np.random.permutation(C)[:U]
    fk = mx_kscale(K)
    ff = mx_kscale(F)
    fr = mx_kscale(R)
    xtp = pack_weight(n((K, T)) / fk[:, None], "e4m3")
    xop = pack_weight(n((F, Z)) / ff[:, None], "e2m1")
    wp = pack_weight(n((K, R)) * 1 / np.sqrt(K) * fk[:, None], "e2m1")
    w0p = pack_weight(n((F, R)) * 1 / np.sqrt(F) * ff[:, None], "e4m3")
    return {
        "xt_words": xtp[0],
        "xt_scales": xtp[1],
        "xo_words": xop[0],
        "xo_scales": xop[1],
        "w_words": wp[0],
        "w_scales": wp[1],
        "w0_words": w0p[0],
        "w0_scales": w0p[1],
        "en": (0.6 * n((R, S))).astype(np.float32),
        "sg": (0.25 * sgn((R, 1))).astype(np.float32),
        "lo": (np.random.uniform(-0.4, 0.4, (R, 1)) + np.log(fr)[:, None]).astype(np.float32),
        "sa": (sgn((R, 1)) / fr[:, None] / np.sqrt(R)).astype(np.float32),
        "offs": striped(idx),
        "offs2": striped(idx2),
        "offs3": striped(idx3),
        "offs4": striped(idx4),
        "offs5": striped(idx5),
    }


def reference(xt_words, xt_scales, xo_words, xo_scales, w_words, w_scales, w0_words, w0_scales, en, sg, lo, sa, offs, offs2, offs3, offs4, offs5):
    idx = unstriped(offs)
    idx2 = unstriped(offs2)
    idx3 = unstriped(offs3)
    idx4 = unstriped(offs4)
    idx5 = unstriped(offs5)
    xtu = unpack_weight(xt_words, xt_scales, "e4m3")
    xou = unpack_weight(xo_words, xo_scales, "e2m1")
    wu = unpack_weight(w_words, w_scales, "e2m1")
    w0u = unpack_weight(w0_words, w0_scales, "e4m3")
    xtidxg = xtu[:, idx]
    xoidx2g = xou[:, idx2]
    a = wu.T @ xtidxg + w0u.T @ xoidx2g
    pw = np.zeros((R, C))
    pw[:, idx3] = a * f64(sa)
    z1 = np.exp(f64(en)[:, idx4] * f64(sg) + f64(lo))
    z2 = pw[:, idx5]
    z1q = mxq(z1, 0, "e4m3")
    z2q = mxq(z2, 0, "e4m3")
    y = z1q.T @ z2q
    return y

@@ -1,0 +1,137 @@
+from contextlib import ExitStack
+
+import concourse.mybir as mybir
+
+F32 = mybir.dt.float32
+BF16 = mybir.dt.bfloat16
+I32 = mybir.dt.int32
+U32 = mybir.dt.uint32
+U16 = mybir.dt.uint16
+U8 = mybir.dt.uint8
+E4M3 = mybir.dt.float8_e4m3fn_x4
+E2M1 = mybir.dt.float4_e2m1fn_x4
+ACT = mybir.ActivationFunctionType
+
+P = 128
+PACK = 4
+T, J, R, Z, C, S, O, U = 1024, 256, 512, 1024, 512, 512, 128, 128
+FLOPS = 285212672
+
+
+def tile_list_energyresults_kernel(tc, xt_words, xt_scales, xo_words, xo_scales, w_words, w_scales,
+                                       w0_words, w0_scales, en, sg, lo, sa, offs, offs2, offs3, offs4, offs5, out):
+    nc = tc.nc
+    with ExitStack() as ctx:
+        sb = ctx.enter_context(tc.tile_pool(name="sb", bufs=1))
+        ps = ctx.enter_context(tc.psum_pool(name="ps", bufs=1))
+
+        def tile(name, cols, dtype):
+            return sb.tile([P, cols], dtype, name=name, align_bytes=64)
+
+        l1 = tile("l1", J // 16, U16)
+        l2 = tile("l2", J // 16, U16)
+        l3 = tile("l3", J // 16, U16)
+        l4 = tile("l4", O // 16, U16)
+        l5 = tile("l5", U // 16, U16)
+        xt_w = tile("xt_w", T, U32)
+        xo_w = tile("xo_w", Z, U16)
+        xt_s = tile("xt_s", T, U8)
+        xo_s = tile("xo_s", Z, U8)
+        w_w = tile("w_w", R, U16)
+        w0_w = tile("w0_w", R, U32)
+        w_s = tile("w_s", 2 * R, U8)
+        w0_s = tile("w0_s", 2 * R, U8)
+        en_t = [tile("en%d" % t, S, F32) for t in range(PACK)]
+        pw = [tile("pw%d" % t, C, F32) for t in range(PACK)]
+        sg_t = tile("sg_t", PACK, F32)
+        lo_t = tile("lo_t", PACK, F32)
+        sa_t = tile("sa_t", PACK, F32)
+
+        for plane in (xt_s, w_s, xo_s, w0_s):
+            nc.vector.memset(plane[:].bitcast(I32), 0)
+
+        def load_plane(queue, plane, scales):
+            for q in range(4):
+                queue.dma_start(plane[32 * q : 32 * q + 4, :].bitcast(I32), scales[0, 4 * q : 4 * q + 4, :].bitcast(I32))
+
+        def load_half_planes(queue, plane, scales):
+            rows = scales[0].bitcast(I32).rearrange("(h q r) c -> q r h c", h=2, q=2)
+            for q in range(2):
+                queue.dma_start(plane[32 * q : 32 * q + 4, :].bitcast(I32).rearrange("r (h c) -> r h c", h=2), rows[q])
+
+        def per_row(v):
+            return v.rearrange("(p t) o -> p (t o)", t=PACK)
+
+        en_rows = en.rearrange("(p t) s -> t p s", t=PACK)
+
+        nc.sync.dma_start(xt_w[:].bitcast(I32), xt_words[0].rearrange("p c r -> p (c r)").bitcast(I32))
+        nc.sync.dma_start(l1[:], offs)
+        nc.sync.dma_start(l2[:], offs2)
+        load_plane(nc.sync, xt_s, xt_scales)
+        nc.sync.dma_start(xo_w[:].bitcast(I32), xo_words[0].bitcast(I32))
+        nc.sync.dma_start(w0_w[:].bitcast(I32), w0_words[0].rearrange("p c r -> p (c r)").bitcast(I32))
+        load_plane(nc.sync, xo_s, xo_scales)
+        load_half_planes(nc.sync, w0_s, w0_scales)
+        nc.sync.dma_start(w_w[:].bitcast(I32), w_words[0].bitcast(I32))
+        load_half_planes(nc.gpsimd, w_s, w_scales)
+        nc.gpsimd.dma_start(sa_t[:], per_row(sa))
+        nc.gpsimd.dma_start(sg_t[:], per_row(sg))
+        nc.gpsimd.dma_start(lo_t[:], per_row(lo))
+        nc.sync.dma_start(l3[:], offs3)
+        nc.sync.dma_start(en_t[0][:], en_rows[0])
+        nc.sync.dma_start(l4[:], offs4)
+        for t in range(1, PACK):
+            nc.sync.dma_start(en_t[t][:], en_rows[t])
+        nc.sync.dma_start(l5[:], offs5)
+
+        for t in range(PACK):
+            nc.vector.memset(pw[t][:], 0.0)
+
+        xt_gw = tile("xt_gw", J, U32)
+        xt_gs = tile("xt_gs", J, U8)
+        xo_gw = tile("xo_gw", J, U16)
+        xo_gs = tile("xo_gs", J, U8)
+        nc.vector.tensor_copy(xt_gs[:], xt_s[:].indirect(l1[:]))
+        nc.vector.tensor_copy(xt_gw[:], xt_w[:].indirect(l1[:]))
+        nc.vector.tensor_copy(xo_gw[:], xo_w[:].indirect(l2[:]))
+        nc.vector.tensor_copy(xo_gs[:], xo_s[:].indirect(l2[:]))
+
+        for plane in (w_s, w0_s):
+            words = plane[:].bitcast(I32)
+            nc.vector.tensor_copy(words[64:128, 0 : R // 4], words[0:64, R // 4 : R // 2])
+
+        z1 = tile("z1", PACK * O, BF16)
+        z2 = tile("z2", PACK * U, BF16)
+        for t in range(PACK):
+            w_pw = tile("w_pw%d" % t, P, U16)
+            w_ps = tile("w_ps%d" % t, P, U8)
+            w0_pw = tile("w0_pw%d" % t, P, U32)
+            w0_ps = tile("w0_ps%d" % t, P, U8)
+            nc.vector.tensor_copy(w0_ps[:], w0_s[:, t:R:PACK])
+            nc.vector.tensor_copy(w_ps[:], w_s[:, t:R:PACK])
+            nc.vector.tensor_copy(w0_pw[:].bitcast(I32), w0_w[:].bitcast(I32)[:, t:R:PACK])
+            nc.vector.tensor_copy(w_pw[:], w_w[:, t:R:PACK])
+            acc = ps.tile([P, J], F32, name="acc%d" % t)
+            nc.tensor.matmul_mx(out=acc[:], lhsT=w0_pw[:].bitcast(E4M3), lhsT_scale=w0_ps[:],
+                                rhs=xo_gw[:].bitcast(E2M1), rhs_scale=xo_gs[:], start=True, stop=False)
+            nc.tensor.matmul_mx(out=acc[:], lhsT=w_pw[:].bitcast(E2M1), lhsT_scale=w_ps[:],
+                                rhs=xt_gw[:].bitcast(E4M3), rhs_scale=xt_gs[:], start=False, stop=True)
+            a_t = tile("a%d" % t, J, F32)
+            nc.vector.tensor_copy(a_t[:], acc[:])
+            nc.scalar.activation(out=z1[:, t : PACK * O : PACK], in_=en_t[t][:].indirect(l4[:]), func=ACT.Exp,
+                                 bias=lo_t[:, t : t + 1], scale=sg_t[:, t : t + 1])
+            nc.scalar.activation(out=pw[t][:].indirect(l3[:]), in_=a_t[:], func=ACT.Copy, scale=sa_t[:, t : t + 1])
+            nc.scalar.activation(out=z2[:, t : PACK * U : PACK], in_=pw[t][:].indirect(l5[:]), func=ACT.Copy)
+
+        z1_w = tile("z1_w", O, U32)
+        z1_s = tile("z1_s", O, U8)
+        z2_w = tile("z2_w", U, U32)
+        z2_s = tile("z2_s", U, U8)
+        nc.vector.quantize_mx(out=z1_w[:].bitcast(E4M3), scales=z1_s[:], in_=z1[:])
+        nc.vector.quantize_mx(out=z2_w[:].bitcast(E4M3), scales=z2_s[:], in_=z2[:])
+        score = ps.tile([O, U], F32, name="score")
+        nc.tensor.matmul_mx(out=score[:], lhsT=z1_w[:].bitcast(E4M3), lhsT_scale=z1_s[:],
+                            rhs=z2_w[:].bitcast(E4M3), rhs_scale=z2_s[:], start=True, stop=True)
+        res = tile("res", U, F32)
+        nc.vector.tensor_copy(res[:], score[:])
+        nc.sync.dma_start(out, res[:])

@@ -15,6 +15,7 @@ ACT = mybir.ActivationFunctionType
 P = 128
 PACK = 4
 T, J, R, Z, C, S, O, U = 1024, 256, 512, 1024, 512, 512, 128, 128
+H = J // 2
 FLOPS = 285212672
 
 
@@ -23,10 +24,11 @@ def tile_list_energyresults_kernel(tc, xt_words, xt_scales, xo_words, xo_scales,
     nc = tc.nc
     with ExitStack() as ctx:
         sb = ctx.enter_context(tc.tile_pool(name="sb", bufs=1))
+        shared = ctx.enter_context(tc.tile_pool(name="shared", bufs=1))
         ps = ctx.enter_context(tc.psum_pool(name="ps", bufs=1))
 
-        def tile(name, cols, dtype):
-            return sb.tile([P, cols], dtype, name=name, align_bytes=64)
+        def tile(name, cols, dtype, rows=P):
+            return sb.tile([rows, cols], dtype, name=name, align_bytes=64)
 
         l1 = tile("l1", J // 16, U16)
         l2 = tile("l2", J // 16, U16)
@@ -35,7 +37,8 @@ def tile_list_energyresults_kernel(tc, xt_words, xt_scales, xo_words, xo_scales,
         l5 = tile("l5", U // 16, U16)
         xt_w = tile("xt_w", T, U32)
         xo_w = tile("xo_w", Z, U16)
-        xt_s = tile("xt_s", T, U8)
+        xt_s = shared.tile([P, T], U8, name="xt_s", align_bytes=64, offset=0)
+        xo_st = tile("xo_st", 2 * Z, U8, rows=64)
         xo_s = tile("xo_s", Z, U8)
         w_w = tile("w_w", R, U16)
         w0_w = tile("w0_w", R, U32)
@@ -47,91 +50,146 @@ def tile_list_energyresults_kernel(tc, xt_words, xt_scales, xo_words, xo_scales,
         lo_t = tile("lo_t", PACK, F32)
         sa_t = tile("sa_t", PACK, F32)
 
-        for plane in (xt_s, w_s, xo_s, w0_s):
+        for plane in (w0_s, xo_st, w_s, xt_s):
             nc.vector.memset(plane[:].bitcast(I32), 0)
 
-        def load_plane(queue, plane, scales):
-            for q in range(4):
-                queue.dma_start(plane[32 * q : 32 * q + 4, :].bitcast(I32), scales[0, 4 * q : 4 * q + 4, :].bitcast(I32))
+        def load_quarter(plane, scales, q):
+            nc.sync.dma_start(plane[32 * q : 32 * q + 4, :].bitcast(I32), scales[0, 4 * q : 4 * q + 4, :].bitcast(I32))
 
-        def load_half_planes(queue, plane, scales):
+        def load_half_plane(plane, scales, first, q):
             rows = scales[0].bitcast(I32).rearrange("(h q r) c -> q r h c", h=2, q=2)
-            for q in range(2):
-                queue.dma_start(plane[32 * q : 32 * q + 4, :].bitcast(I32).rearrange("r (h c) -> r h c", h=2), rows[q])
+            part = plane[first + 32 * q : first + 32 * q + 4, :].bitcast(I32).rearrange("r (h c) -> r h c", h=2)
+            nc.sync.dma_start(part, rows[q])
 
         def per_row(v):
             return v.rearrange("(p t) o -> p (t o)", t=PACK)
 
         en_rows = en.rearrange("(p t) s -> t p s", t=PACK)
 
-        nc.sync.dma_start(xt_w[:].bitcast(I32), xt_words[0].rearrange("p c r -> p (c r)").bitcast(I32))
-        nc.sync.dma_start(l1[:], offs)
         nc.sync.dma_start(l2[:], offs2)
-        load_plane(nc.sync, xt_s, xt_scales)
-        nc.sync.dma_start(xo_w[:].bitcast(I32), xo_words[0].bitcast(I32))
-        nc.sync.dma_start(w0_w[:].bitcast(I32), w0_words[0].rearrange("p c r -> p (c r)").bitcast(I32))
-        load_plane(nc.sync, xo_s, xo_scales)
-        load_half_planes(nc.sync, w0_s, w0_scales)
+        nc.sync.dma_start(l1[:], offs)
         nc.sync.dma_start(w_w[:].bitcast(I32), w_words[0].bitcast(I32))
-        load_half_planes(nc.gpsimd, w_s, w_scales)
-        nc.gpsimd.dma_start(sa_t[:], per_row(sa))
-        nc.gpsimd.dma_start(sg_t[:], per_row(sg))
-        nc.gpsimd.dma_start(lo_t[:], per_row(lo))
+        nc.sync.dma_start(xo_w[:].bitcast(I32), xo_words[0].bitcast(I32))
+        for q in range(2):
+            load_half_plane(w0_s, w0_scales, 0, q)
+        for q in range(2):
+            load_half_plane(xo_st, xo_scales, 0, q)
+        for q in range(2):
+            load_half_plane(w_s, w_scales, 64, q)
+        nc.sync.dma_start(xt_w[:].bitcast(I32), xt_words[0].rearrange("p c r -> p (c r)").bitcast(I32))
+        nc.sync.dma_start(w0_w[:].bitcast(I32), w0_words[0].rearrange("p c r -> p (c r)").bitcast(I32))
+        for q in range(4):
+            load_quarter(xt_s, xt_scales, q)
         nc.sync.dma_start(l3[:], offs3)
-        nc.sync.dma_start(en_t[0][:], en_rows[0])
+        nc.sync.dma_start(sa_t[:], per_row(sa))
         nc.sync.dma_start(l4[:], offs4)
+        nc.sync.dma_start(en_t[0][:], en_rows[0])
+        nc.sync.dma_start(sg_t[:], per_row(sg))
+        nc.sync.dma_start(lo_t[:], per_row(lo))
         for t in range(1, PACK):
             nc.sync.dma_start(en_t[t][:], en_rows[t])
         nc.sync.dma_start(l5[:], offs5)
 
         for t in range(PACK):
-            nc.vector.memset(pw[t][:], 0.0)
+            (nc.vector if t < 2 else nc.gpsimd).memset(pw[t][:], 0.0)
 
-        xt_gw = tile("xt_gw", J, U32)
-        xt_gs = tile("xt_gs", J, U8)
-        xo_gw = tile("xo_gw", J, U16)
-        xo_gs = tile("xo_gs", J, U8)
-        nc.vector.tensor_copy(xt_gs[:], xt_s[:].indirect(l1[:]))
-        nc.vector.tensor_copy(xt_gw[:], xt_w[:].indirect(l1[:]))
-        nc.vector.tensor_copy(xo_gw[:], xo_w[:].indirect(l2[:]))
-        nc.vector.tensor_copy(xo_gs[:], xo_s[:].indirect(l2[:]))
+        xt_gw = [tile("xt_gw0", H, U32), shared.tile([P, H], U32, name="xt_gw1", align_bytes=64, offset=0)]
+        xo_gw = [tile("xo_gw0", H, U16), shared.tile([P, H], U16, name="xo_gw1", align_bytes=64, offset=5 * H)]
+        xt_gs = [tile("xt_gs%d" % h, H, U8) for h in range(2)]
+        xo_gs = [tile("xo_gs0", H, U8), shared.tile([P, H], U8, name="xo_gs1", align_bytes=64, offset=4 * H)]
 
-        for plane in (w_s, w0_s):
-            words = plane[:].bitcast(I32)
-            nc.vector.tensor_copy(words[64:128, 0 : R // 4], words[0:64, R // 4 : R // 2])
+        def gather(dst, src, lst, h):
+            nc.vector.tensor_copy(dst[h][:], src[:].indirect(lst[:, H // 16 * h : H // 16 * (h + 1)]))
+
+        w0_pw = tile("w0_pw", R, U32)
+        w_pw = tile("w_pw", R, U16)
+        gather(xo_gw, xo_w, l2, 0)
+        nc.scalar.copy(w0_pw[:, 0:P], w0_w[:, 0:R:PACK])
+        nc.scalar.copy(w0_pw[:, P:R].rearrange("p (t m) -> p m t", t=PACK - 1),
+                       w0_w[:].rearrange("p (m t) -> p m t", t=PACK)[:, :, 1:PACK])
+        for h in range(2):
+            nc.vector.tensor_copy(xo_s[:].bitcast(I32)[64 * h : 64 * (h + 1), :],
+                                  xo_st[:].bitcast(I32)[:, Z // 4 * h : Z // 4 * (h + 1)])
+        nc.vector.tensor_copy(w_pw[:].rearrange("p (t m) -> p t m", t=PACK), w_w[:].rearrange("p (m t) -> p t m", t=PACK))
+        w0_words32 = w0_s[:].bitcast(I32)
+        nc.vector.tensor_copy(w0_words32[64:128, 0 : R // 4], w0_words32[0:64, R // 4 : R // 2])
+        w_words32 = w_s[:].bitcast(I32)
+        nc.vector.tensor_copy(w_words32[0:64, R // 4 : R // 2], w_words32[64:128, 0 : R // 4])
+        gather(xt_gw, xt_w, l1, 0)
+        gather(xo_gs, xo_s, l2, 0)
+        gather(xt_gs, xt_s, l1, 0)
 
         z1 = tile("z1", PACK * O, BF16)
         z2 = tile("z2", PACK * U, BF16)
-        for t in range(PACK):
-            w_pw = tile("w_pw%d" % t, P, U16)
-            w_ps = tile("w_ps%d" % t, P, U8)
-            w0_pw = tile("w0_pw%d" % t, P, U32)
-            w0_ps = tile("w0_ps%d" % t, P, U8)
-            nc.vector.tensor_copy(w0_ps[:], w0_s[:, t:R:PACK])
-            nc.vector.tensor_copy(w_ps[:], w_s[:, t:R:PACK])
-            nc.vector.tensor_copy(w0_pw[:].bitcast(I32), w0_w[:].bitcast(I32)[:, t:R:PACK])
-            nc.vector.tensor_copy(w_pw[:], w_w[:, t:R:PACK])
-            acc = ps.tile([P, J], F32, name="acc%d" % t)
-            nc.tensor.matmul_mx(out=acc[:], lhsT=w0_pw[:].bitcast(E4M3), lhsT_scale=w0_ps[:],
-                                rhs=xo_gw[:].bitcast(E2M1), rhs_scale=xo_gs[:], start=True, stop=False)
-            nc.tensor.matmul_mx(out=acc[:], lhsT=w_pw[:].bitcast(E2M1), lhsT_scale=w_ps[:],
-                                rhs=xt_gw[:].bitcast(E4M3), rhs_scale=xt_gs[:], start=False, stop=True)
-            a_t = tile("a%d" % t, J, F32)
-            nc.vector.tensor_copy(a_t[:], acc[:])
+        w_ps = [tile("w_ps%d" % t, P, U8) for t in range(PACK)]
+        w0_ps = [tile("w0_ps%d" % t, P, U8) for t in range(PACK)]
+
+        def deal(t):
+            nc.vector.tensor_copy(w0_ps[t][:], w0_s[:, t:R:PACK])
+            nc.vector.tensor_copy(w_ps[t][:], w_s[:, R + t : 2 * R : PACK])
+
+        def product(t, h):
+            acc = ps.tile([P, H], F32, name="acc", bufs=6)
+            nc.tensor.matmul_mx(out=acc[:], lhsT=w0_pw[:, P * t : P * (t + 1)].bitcast(E4M3), lhsT_scale=w0_ps[t][:],
+                                rhs=xo_gw[h][:].bitcast(E2M1), rhs_scale=xo_gs[h][:], start=True, stop=False)
+            nc.tensor.matmul_mx(out=acc[:], lhsT=w_pw[:, P * t : P * (t + 1)].bitcast(E2M1), lhsT_scale=w_ps[t][:],
+                                rhs=xt_gw[h][:].bitcast(E4M3), rhs_scale=xt_gs[h][:], start=False, stop=True)
+            return acc
+
+        def put(t, h, acc):
+            a_t = tile("a%d_%d" % (t, h), H, F32)
+            if (t, h) == (0, 0):
+                nc.scalar.activation(out=a_t[:], in_=acc[:], func=ACT.Copy)
+            else:
+                nc.vector.tensor_copy(a_t[:], acc[:])
+            nc.scalar.activation(out=pw[t][:].indirect(l3[:, H // 16 * h : H // 16 * (h + 1)]), in_=a_t[:],
+                                 func=ACT.Copy, scale=sa_t[:, t : t + 1])
+
+        def look(t):
             nc.scalar.activation(out=z1[:, t : PACK * O : PACK], in_=en_t[t][:].indirect(l4[:]), func=ACT.Exp,
                                  bias=lo_t[:, t : t + 1], scale=sg_t[:, t : t + 1])
-            nc.scalar.activation(out=pw[t][:].indirect(l3[:]), in_=a_t[:], func=ACT.Copy, scale=sa_t[:, t : t + 1])
-            nc.scalar.activation(out=z2[:, t : PACK * U : PACK], in_=pw[t][:].indirect(l5[:]), func=ACT.Copy)
 
+        def pick(t, lo_u=0, hi_u=U):
+            nc.scalar.activation(out=z2[:, PACK * lo_u + t : PACK * hi_u : PACK],
+                                 in_=pw[t][:].indirect(l5[:, lo_u // 16 : hi_u // 16]), func=ACT.Copy)
+
+        deal(0)
+        acc = product(0, 0)
+        for t in range(PACK):
+            if t + 1 < PACK:
+                deal(t + 1)
+                nxt = product(t + 1, 0)
+            put(t, 0, acc)
+            acc = nxt
+        gather(xt_gs, xt_s, l1, 1)
+        gather(xo_gw, xo_w, l2, 1)
+        gather(xo_gs, xo_s, l2, 1)
+        gather(xt_gw, xt_w, l1, 1)
+        for t in range(PACK):
+            look(t)
         z1_w = tile("z1_w", O, U32)
         z1_s = tile("z1_s", O, U8)
         z2_w = tile("z2_w", U, U32)
         z2_s = tile("z2_s", U, U8)
+        for t in range(PACK):
+            put(t, 1, product(t, 1))
+            if t > 0:
+                pick(t - 1)
+
         nc.vector.quantize_mx(out=z1_w[:].bitcast(E4M3), scales=z1_s[:], in_=z1[:])
-        nc.vector.quantize_mx(out=z2_w[:].bitcast(E4M3), scales=z2_s[:], in_=z2[:])
-        score = ps.tile([O, U], F32, name="score")
-        nc.tensor.matmul_mx(out=score[:], lhsT=z1_w[:].bitcast(E4M3), lhsT_scale=z1_s[:],
-                            rhs=z2_w[:].bitcast(E4M3), rhs_scale=z2_s[:], start=True, stop=True)
-        res = tile("res", U, F32)
-        nc.vector.tensor_copy(res[:], score[:])
-        nc.sync.dma_start(out, res[:])
+        for u0 in (0, U // 2):
+            cols = slice(u0, u0 + U // 2)
+            pick(PACK - 1, cols.start, cols.stop)
+            nc.vector.quantize_mx(out=z2_w[:, cols].bitcast(E4M3), scales=z2_s[:, cols],
+                                  in_=z2[:, PACK * cols.start : PACK * cols.stop])
+        for u0 in (0, U // 2):
+            cols = slice(u0, u0 + U // 2)
+            score = ps.tile([O, U // 2], F32, name="score", bufs=2)
+            nc.tensor.matmul_mx(out=score[:], lhsT=z1_w[:].bitcast(E4M3), lhsT_scale=z1_s[:],
+                                rhs=z2_w[:, cols].bitcast(E4M3), rhs_scale=z2_s[:, cols], start=True, stop=True)
+            res = tile("res%d" % u0, U // 2, F32)
+            if u0 == 0:
+                nc.vector.tensor_copy(res[:], score[:])
+            else:
+                nc.scalar.copy(res[:], score[:])
+            nc.sync.dma_start(out[:, cols], res[:])

@@ -16,6 +16,7 @@ P = 128
 PACK = 4
 T, J, R, Z, C, S, O, U = 1024, 256, 512, 1024, 512, 512, 128, 128
 H = J // 2
+EARLY = 2
 FLOPS = 285212672
 
 
@@ -66,32 +67,34 @@ def tile_list_energyresults_kernel(tc, xt_words, xt_scales, xo_words, xo_scales,
 
         en_rows = en.rearrange("(p t) s -> t p s", t=PACK)
 
+        nc.gpsimd.dma_start(sg_t[:], per_row(sg))
+        nc.gpsimd.dma_start(lo_t[:], per_row(lo))
+        for t in range(EARLY):
+            nc.gpsimd.dma_start(en_t[t][:], en_rows[t])
+
         nc.sync.dma_start(l2[:], offs2)
         nc.sync.dma_start(l1[:], offs)
-        nc.sync.dma_start(w_w[:].bitcast(I32), w_words[0].bitcast(I32))
+        nc.sync.dma_start(w0_w[:].bitcast(I32), w0_words[0].rearrange("p c r -> p (c r)").bitcast(I32))
         nc.sync.dma_start(xo_w[:].bitcast(I32), xo_words[0].bitcast(I32))
         for q in range(2):
             load_half_plane(w0_s, w0_scales, 0, q)
         for q in range(2):
             load_half_plane(xo_st, xo_scales, 0, q)
-        for q in range(2):
-            load_half_plane(w_s, w_scales, 64, q)
+        nc.sync.dma_start(l4[:], offs4)
+        load_half_plane(w_s, w_scales, 64, 0)
         nc.sync.dma_start(xt_w[:].bitcast(I32), xt_words[0].rearrange("p c r -> p (c r)").bitcast(I32))
-        nc.sync.dma_start(w0_w[:].bitcast(I32), w0_words[0].rearrange("p c r -> p (c r)").bitcast(I32))
+        nc.sync.dma_start(w_w[:].bitcast(I32), w_words[0].bitcast(I32))
+        load_half_plane(w_s, w_scales, 64, 1)
         for q in range(4):
             load_quarter(xt_s, xt_scales, q)
         nc.sync.dma_start(l3[:], offs3)
         nc.sync.dma_start(sa_t[:], per_row(sa))
-        nc.sync.dma_start(l4[:], offs4)
-        nc.sync.dma_start(en_t[0][:], en_rows[0])
-        nc.sync.dma_start(sg_t[:], per_row(sg))
-        nc.sync.dma_start(lo_t[:], per_row(lo))
-        for t in range(1, PACK):
+        for t in range(EARLY, PACK):
             nc.sync.dma_start(en_t[t][:], en_rows[t])
         nc.sync.dma_start(l5[:], offs5)
 
         for t in range(PACK):
-            (nc.vector if t < 2 else nc.gpsimd).memset(pw[t][:], 0.0)
+            nc.vector.memset(pw[t][:], 0.0)
 
         xt_gw = [tile("xt_gw0", H, U32), shared.tile([P, H], U32, name="xt_gw1", align_bytes=64, offset=0)]
         xo_gw = [tile("xo_gw0", H, U16), shared.tile([P, H], U16, name="xo_gw1", align_bytes=64, offset=5 * H)]
@@ -104,9 +107,7 @@ def tile_list_energyresults_kernel(tc, xt_words, xt_scales, xo_words, xo_scales,
         w0_pw = tile("w0_pw", R, U32)
         w_pw = tile("w_pw", R, U16)
         gather(xo_gw, xo_w, l2, 0)
-        nc.scalar.copy(w0_pw[:, 0:P], w0_w[:, 0:R:PACK])
-        nc.scalar.copy(w0_pw[:, P:R].rearrange("p (t m) -> p m t", t=PACK - 1),
-                       w0_w[:].rearrange("p (m t) -> p m t", t=PACK)[:, :, 1:PACK])
+        nc.scalar.copy(w0_pw[:].rearrange("p (t m) -> p m t", t=PACK), w0_w[:].rearrange("p (m t) -> p m t", t=PACK))
         for h in range(2):
             nc.vector.tensor_copy(xo_s[:].bitcast(I32)[64 * h : 64 * (h + 1), :],
                                   xo_st[:].bitcast(I32)[:, Z // 4 * h : Z // 4 * (h + 1)])

from contextlib import ExitStack

import concourse.mybir as mybir

F32 = mybir.dt.float32
BF16 = mybir.dt.bfloat16
I32 = mybir.dt.int32
U32 = mybir.dt.uint32
U16 = mybir.dt.uint16
U8 = mybir.dt.uint8
E4M3 = mybir.dt.float8_e4m3fn_x4
E2M1 = mybir.dt.float4_e2m1fn_x4
ACT = mybir.ActivationFunctionType

P = 128
PACK = 4
T, J, R, Z, C, S, O, U = 1024, 256, 512, 1024, 512, 512, 128, 128
H = J // 2
EARLY = 2
FLOPS = 285212672


def tile_list_energyresults_kernel(tc, xt_words, xt_scales, xo_words, xo_scales, w_words, w_scales,
                                       w0_words, w0_scales, en, sg, lo, sa, offs, offs2, offs3, offs4, offs5, out):
    nc = tc.nc
    with ExitStack() as ctx:
        sb = ctx.enter_context(tc.tile_pool(name="sb", bufs=1))
        shared = ctx.enter_context(tc.tile_pool(name="shared", bufs=1))
        ps = ctx.enter_context(tc.psum_pool(name="ps", bufs=1))

        def tile(name, cols, dtype, rows=P):
            return sb.tile([rows, cols], dtype, name=name, align_bytes=64)

        l1 = tile("l1", J // 16, U16)
        l2 = tile("l2", J // 16, U16)
        l3 = tile("l3", J // 16, U16)
        l4 = tile("l4", O // 16, U16)
        l5 = tile("l5", U // 16, U16)
        xt_w = tile("xt_w", T, U32)
        xo_w = tile("xo_w", Z, U16)
        xt_s = shared.tile([P, T], U8, name="xt_s", align_bytes=64, offset=0)
        xo_st = tile("xo_st", 2 * Z, U8, rows=64)
        xo_s = tile("xo_s", Z, U8)
        w_w = tile("w_w", R, U16)
        w0_w = tile("w0_w", R, U32)
        w_s = tile("w_s", 2 * R, U8)
        w0_s = tile("w0_s", 2 * R, U8)
        en_t = [tile("en%d" % t, S, F32) for t in range(PACK)]
        pw = [tile("pw%d" % t, C, F32) for t in range(PACK)]
        sg_t = tile("sg_t", PACK, F32)
        lo_t = tile("lo_t", PACK, F32)
        sa_t = tile("sa_t", PACK, F32)

        for plane in (w0_s, xo_st, w_s, xt_s):
            nc.vector.memset(plane[:].bitcast(I32), 0)

        def load_quarter(plane, scales, q):
            nc.sync.dma_start(plane[32 * q : 32 * q + 4, :].bitcast(I32), scales[0, 4 * q : 4 * q + 4, :].bitcast(I32))

        def load_half_plane(plane, scales, first, q):
            rows = scales[0].bitcast(I32).rearrange("(h q r) c -> q r h c", h=2, q=2)
            part = plane[first + 32 * q : first + 32 * q + 4, :].bitcast(I32).rearrange("r (h c) -> r h c", h=2)
            nc.sync.dma_start(part, rows[q])

        def per_row(v):
            return v.rearrange("(p t) o -> p (t o)", t=PACK)

        en_rows = en.rearrange("(p t) s -> t p s", t=PACK)

        nc.gpsimd.dma_start(sg_t[:], per_row(sg))
        nc.gpsimd.dma_start(lo_t[:], per_row(lo))
        for t in range(EARLY):
            nc.gpsimd.dma_start(en_t[t][:], en_rows[t])

        nc.sync.dma_start(l2[:], offs2)
        nc.sync.dma_start(l1[:], offs)
        nc.sync.dma_start(w0_w[:].bitcast(I32), w0_words[0].rearrange("p c r -> p (c r)").bitcast(I32))
        nc.sync.dma_start(xo_w[:].bitcast(I32), xo_words[0].bitcast(I32))
        for q in range(2):
            load_half_plane(w0_s, w0_scales, 0, q)
        for q in range(2):
            load_half_plane(xo_st, xo_scales, 0, q)
        nc.sync.dma_start(l4[:], offs4)
        load_half_plane(w_s, w_scales, 64, 0)
        nc.sync.dma_start(xt_w[:].bitcast(I32), xt_words[0].rearrange("p c r -> p (c r)").bitcast(I32))
        nc.sync.dma_start(w_w[:].bitcast(I32), w_words[0].bitcast(I32))
        load_half_plane(w_s, w_scales, 64, 1)
        for q in range(4):
            load_quarter(xt_s, xt_scales, q)
        nc.sync.dma_start(l3[:], offs3)
        nc.sync.dma_start(sa_t[:], per_row(sa))
        for t in range(EARLY, PACK):
            nc.sync.dma_start(en_t[t][:], en_rows[t])
        nc.sync.dma_start(l5[:], offs5)

        for t in range(PACK):
            nc.vector.memset(pw[t][:], 0.0)

        xt_gw = [tile("xt_gw0", H, U32), shared.tile([P, H], U32, name="xt_gw1", align_bytes=64, offset=0)]
        xo_gw = [tile("xo_gw0", H, U16), shared.tile([P, H], U16, name="xo_gw1", align_bytes=64, offset=5 * H)]
        xt_gs = [tile("xt_gs%d" % h, H, U8) for h in range(2)]
        xo_gs = [tile("xo_gs0", H, U8), shared.tile([P, H], U8, name="xo_gs1", align_bytes=64, offset=4 * H)]

        def gather(dst, src, lst, h):
            nc.vector.tensor_copy(dst[h][:], src[:].indirect(lst[:, H // 16 * h : H // 16 * (h + 1)]))

        w0_pw = tile("w0_pw", R, U32)
        w_pw = tile("w_pw", R, U16)
        gather(xo_gw, xo_w, l2, 0)
        nc.scalar.copy(w0_pw[:].rearrange("p (t m) -> p m t", t=PACK), w0_w[:].rearrange("p (m t) -> p m t", t=PACK))
        for h in range(2):
            nc.vector.tensor_copy(xo_s[:].bitcast(I32)[64 * h : 64 * (h + 1), :],
                                  xo_st[:].bitcast(I32)[:, Z // 4 * h : Z // 4 * (h + 1)])
        nc.vector.tensor_copy(w_pw[:].rearrange("p (t m) -> p t m", t=PACK), w_w[:].rearrange("p (m t) -> p t m", t=PACK))
        w0_words32 = w0_s[:].bitcast(I32)
        nc.vector.tensor_copy(w0_words32[64:128, 0 : R // 4], w0_words32[0:64, R // 4 : R // 2])
        w_words32 = w_s[:].bitcast(I32)
        nc.vector.tensor_copy(w_words32[0:64, R // 4 : R // 2], w_words32[64:128, 0 : R // 4])
        gather(xt_gw, xt_w, l1, 0)
        gather(xo_gs, xo_s, l2, 0)
        gather(xt_gs, xt_s, l1, 0)

        z1 = tile("z1", PACK * O, BF16)
        z2 = tile("z2", PACK * U, BF16)
        w_ps = [tile("w_ps%d" % t, P, U8) for t in range(PACK)]
        w0_ps = [tile("w0_ps%d" % t, P, U8) for t in range(PACK)]

        def deal(t):
            nc.vector.tensor_copy(w0_ps[t][:], w0_s[:, t:R:PACK])
            nc.vector.tensor_copy(w_ps[t][:], w_s[:, R + t : 2 * R : PACK])

        def product(t, h):
            acc = ps.tile([P, H], F32, name="acc", bufs=6)
            nc.tensor.matmul_mx(out=acc[:], lhsT=w0_pw[:, P * t : P * (t + 1)].bitcast(E4M3), lhsT_scale=w0_ps[t][:],
                                rhs=xo_gw[h][:].bitcast(E2M1), rhs_scale=xo_gs[h][:], start=True, stop=False)
            nc.tensor.matmul_mx(out=acc[:], lhsT=w_pw[:, P * t : P * (t + 1)].bitcast(E2M1), lhsT_scale=w_ps[t][:],
                                rhs=xt_gw[h][:].bitcast(E4M3), rhs_scale=xt_gs[h][:], start=False, stop=True)
            return acc

        def put(t, h, acc):
            a_t = tile("a%d_%d" % (t, h), H, F32)
            if (t, h) == (0, 0):
                nc.scalar.activation(out=a_t[:], in_=acc[:], func=ACT.Copy)
            else:
                nc.vector.tensor_copy(a_t[:], acc[:])
            nc.scalar.activation(out=pw[t][:].indirect(l3[:, H // 16 * h : H // 16 * (h + 1)]), in_=a_t[:],
                                 func=ACT.Copy, scale=sa_t[:, t : t + 1])

        def look(t):
            nc.scalar.activation(out=z1[:, t : PACK * O : PACK], in_=en_t[t][:].indirect(l4[:]), func=ACT.Exp,
                                 bias=lo_t[:, t : t + 1], scale=sg_t[:, t : t + 1])

        def pick(t, lo_u=0, hi_u=U):
            nc.scalar.activation(out=z2[:, PACK * lo_u + t : PACK * hi_u : PACK],
                                 in_=pw[t][:].indirect(l5[:, lo_u // 16 : hi_u // 16]), func=ACT.Copy)

        deal(0)
        acc = product(0, 0)
        for t in range(PACK):
            if t + 1 < PACK:
                deal(t + 1)
                nxt = product(t + 1, 0)
            put(t, 0, acc)
            acc = nxt
        gather(xt_gs, xt_s, l1, 1)
        gather(xo_gw, xo_w, l2, 1)
        gather(xo_gs, xo_s, l2, 1)
        gather(xt_gw, xt_w, l1, 1)
        for t in range(PACK):
            look(t)
        z1_w = tile("z1_w", O, U32)
        z1_s = tile("z1_s", O, U8)
        z2_w = tile("z2_w", U, U32)
        z2_s = tile("z2_s", U, U8)
        for t in range(PACK):
            put(t, 1, product(t, 1))
            if t > 0:
                pick(t - 1)

        nc.vector.quantize_mx(out=z1_w[:].bitcast(E4M3), scales=z1_s[:], in_=z1[:])
        for u0 in (0, U // 2):
            cols = slice(u0, u0 + U // 2)
            pick(PACK - 1, cols.start, cols.stop)
            nc.vector.quantize_mx(out=z2_w[:, cols].bitcast(E4M3), scales=z2_s[:, cols],
                                  in_=z2[:, PACK * cols.start : PACK * cols.stop])
        for u0 in (0, U // 2):
            cols = slice(u0, u0 + U // 2)
            score = ps.tile([O, U // 2], F32, name="score", bufs=2)
            nc.tensor.matmul_mx(out=score[:], lhsT=z1_w[:].bitcast(E4M3), lhsT_scale=z1_s[:],
                                rhs=z2_w[:, cols].bitcast(E4M3), rhs_scale=z2_s[:, cols], start=True, stop=True)
            res = tile("res%d" % u0, U // 2, F32)
            if u0 == 0:
                nc.vector.tensor_copy(res[:], score[:])
            else:
                nc.scalar.copy(res[:], score[:])
            nc.sync.dma_start(out[:, cols], res[:])
